import numpy as np
import ml_dtypes


def mxq(x, axis, fmt="e4m3"):
    dtype, down = {"e4m3": (ml_dtypes.float8_e4m3fn, 7), "e5m2": (ml_dtypes.float8_e5m2, 14)}[fmt]
    v = np.moveaxis(np.asarray(x, np.float32).astype(ml_dtypes.bfloat16).astype(np.float64), axis, -1)
    blocks = v.reshape(v.shape[:-1] + (-1, 32))
    amax = np.abs(blocks).max(-1, keepdims=True)
    byte = np.maximum(np.where(amax > 0, np.frexp(amax)[1] - 1 + 127, 0) - down, 1)
    scale = np.exp2(byte - 127.0)
    codes = (blocks / scale).astype(np.float32).astype(dtype).astype(np.float64)
    return np.moveaxis((codes * scale).reshape(v.shape), -1, axis)


WIDE = False


def mx_kscale(k):
    if not WIDE:
        return np.ones(k)
    levels = np.array([10, -10, 5, -5, 0])
    if k % 512:
        return np.exp2(np.random.permutation(np.resize(levels, k // 32))).repeat(32)
    a = np.empty((k // 512, 16))
    for p in range(k // 512):
        a[p, :8] = np.random.permutation(np.resize(levels, 8))
        for g in range(8):
            far = levels[np.abs(levels - a[p, g]) >= 10]
            a[p, g + 8] = far[np.random.randint(len(far))]
    return np.exp2(a.ravel()).repeat(32)


def f64(x):
    return np.asarray(x).astype(np.float64)


def striped(idx):
    return np.tile(idx.reshape(-1, 16).T, (8, 1)).astype(np.uint16)


def unstriped(offs):
    return offs[:16].T.reshape(-1).astype(np.int64)


def striped8(idx):
    return np.concatenate([x.reshape(-1, 16).T for x in idx]).astype(np.uint16)


def runs(offs, k):
    lists = np.stack([offs[16 * r : 16 * r + 16].T.reshape(-1) for r in range(8)]).astype(np.int64)
    return lists[np.arange(k) % 512 // 64]


def pack_weight(w):
    k, n = w.shape
    w = f64(np.asarray(w, np.float32).astype(ml_dtypes.bfloat16)).reshape(k // 32, 32, n)
    amax = np.abs(w).max(1)
    byte = np.clip(np.where(amax > 0, np.frexp(amax)[1] - 1 + 127 - 7, 1), 1, 254)
    scaled = (w * np.exp2(127.0 - byte)[:, None, :]).reshape(k, n).astype(np.float32)
    words = np.ascontiguousarray(scaled.reshape(k // 512, 128, 4, n).transpose(0, 1, 3, 2)).astype(ml_dtypes.float8_e4m3fn).view(np.uint8)
    return words, np.ascontiguousarray(byte.astype(np.uint8).reshape(k // 512, 16, n))


def unpack_weight(words, scales):
    g, p, n, _ = words.shape
    vals = np.ascontiguousarray(words).view(ml_dtypes.float8_e4m3fn).astype(np.float64) * np.repeat(np.exp2(scales.astype(np.float64) - 127.0), 8, axis=1)[..., None]
    return vals.transpose(0, 1, 3, 2).reshape(g * 512, n)


K, T, S, N, H, G = 512, 2048, 512, 512, 512, 2048


def setup_inputs():
    n = np.random.standard_normal
    s = mx_kscale(K)[:, None]
    u = mx_kscale(S)
    packed_xT = pack_weight(n((K, T)) * s)
    packed_dT = pack_weight(n((K, G)) / s)
    return {
        "x_words": packed_xT[0],
        "x_scales": packed_xT[1],
        "w1": (n((K, H)) / np.sqrt(K) / s).astype(np.float32),
        "d_words": packed_dT[0],
        "d_scales": packed_dT[1],
        "gn": (np.random.uniform(0.5, 1.5, (H, 1)) * u[:, None]).astype(np.float32),
        "w2": (n((H, N)) / np.sqrt(H) / u[:, None]).astype(np.float32),
        "tau": np.random.uniform(0.3, 0.9, (N, 1)).astype(np.float32),
        "offs": striped(np.random.permutation(T)[:S]),
        "k1": striped8(np.random.randint(0, G, (8, H))),
        "two": striped(np.random.permutation(T)[:S]),
        "n1": striped(np.random.permutation(S)),
        "n2": striped(np.random.permutation(S)),
        "n3": striped(np.random.permutation(S)),
        "n4": striped(np.random.permutation(S)),
    }


def reference(x_words, x_scales, w1, d_words, d_scales, gn, w2, tau, offs, k1, two, n1, n2, n3, n4):
    xq = unpack_weight(x_words, x_scales)[:, unstriped(offs)]
    y = mxq(f64(w1), 0, "e4m3").T @ xq
    d_k1 = unpack_weight(d_words, d_scales)[np.arange(K)[:, None], runs(k1, K)]
    x_two = unpack_weight(x_words, x_scales)[:, unstriped(two)]
    d = 0.0625 * (d_k1.T @ x_two)
    z = f64(gn) * (0.75 * (y * d[:, unstriped(n2)] - (y[:, unstriped(n1)] * d)))
    h = mxq(f64(w2), 0, "e4m3").T @ mxq(z, 0, "e4m3")
    top = h.max(axis=1, keepdims=True)
    ea = np.exp(f64(tau) * (h[:, unstriped(n3)] - top))
    return np.maximum(h, 2.0 * ea) - (0.5 * h[:, unstriped(n4)])

@@ -1,0 +1,250 @@
+from contextlib import ExitStack
+
+import concourse.mybir as mybir
+
+F32 = mybir.dt.float32
+BF16 = mybir.dt.bfloat16
+I32 = mybir.dt.int32
+U32 = mybir.dt.uint32
+U16 = mybir.dt.uint16
+U8 = mybir.dt.uint8
+FP8X4 = mybir.dt.float8_e4m3fn_x4
+ALU = mybir.AluOpType
+ACT = mybir.ActivationFunctionType
+
+P = 128
+PACK = 4
+WIDTH = 512
+TABLE = 2048
+HALF = WIDTH // 2
+LIST_COLS = WIDTH // 16
+FUSED_TILES = 2
+ADDING_TILES = 2
+FLOPS = 3 * 2 * 512 * 512 * 512
+
+
+def tile_picked_twkeycrossbecl_none_p_kernel(tc, x_words, x_scales, w1, d_words, d_scales, gn, w2, tau, offs, k1, two, n1, n2, n3, n4, out):
+    nc = tc.nc
+    with ExitStack() as ctx:
+        held = ctx.enter_context(tc.tile_pool(name="held", bufs=1))
+        ring = ctx.enter_context(tc.tile_pool(name="ring", bufs=PACK))
+        psum = ctx.enter_context(tc.psum_pool(name="psum", bufs=8))
+
+        def load_list(src, name):
+            tile = held.tile([P, LIST_COLS], U16, name=name)
+            nc.sync.dma_start(tile[:], src)
+            return tile
+
+        def half_cols(half):
+            return slice(half * HALF, (half + 1) * HALF)
+
+        def half_list(tile, half):
+            return tile[:, half * LIST_COLS // 2 : (half + 1) * LIST_COLS // 2]
+
+        def load_words(src, name):
+            tile = held.tile([P, TABLE], U32, name=name, align_bytes=64)
+            nc.sync.dma_start(tile[:].bitcast(I32), src[0].rearrange("p n t -> p (n t)").bitcast(I32))
+            return tile
+
+        def gather(window, offsets, dtype, name):
+            tile = held.tile([P, WIDTH], dtype, name=name, align_bytes=64)
+            nc.vector.tensor_copy(tile[:], window[:].indirect(offsets[:]))
+            return tile
+
+        def deal(src, dtype, name):
+            tile = held.tile([P, WIDTH], dtype, name=name, align_bytes=64)
+            nc.vector.tensor_copy(
+                tile[:].rearrange("p (t m) -> p m t", t=PACK),
+                src[:].rearrange("p (m t) -> p m t", t=PACK),
+            )
+            return tile
+
+        def load_weight_half(w, half):
+            raw = held.tile([P, PACK, HALF], F32, name=f"w_raw{half}")
+            nc.sync.dma_start(raw[:], w[:, half_cols(half)].rearrange("(p j) c -> p j c", j=PACK))
+            return raw
+
+        def round_weight_half(raw, grouped, half):
+            span = P // 2
+            nc.scalar.copy(
+                grouped[:].rearrange("p (t m j) -> p m j t", t=PACK, j=PACK)[:, half * span : (half + 1) * span],
+                raw[:].rearrange("p j (m t) -> p m j t", t=PACK),
+            )
+
+        def quantize(src, width, name):
+            codes = held.tile([P, width], U32, name=name + "_codes", align_bytes=64)
+            scales = held.tile([P, width], U8, name=name + "_scales", align_bytes=64)
+            nc.vector.quantize_mx(out=codes[:].bitcast(FP8X4), scales=scales[:], in_=src[:])
+            return codes, scales
+
+        def product(acc, left, t, right):
+            cols = slice(t * P, (t + 1) * P)
+            nc.tensor.matmul_mx(
+                out=acc,
+                lhsT=left[0][:, cols].bitcast(FP8X4),
+                lhsT_scale=left[1][:, cols],
+                rhs=right[0][:].bitcast(FP8X4),
+                rhs_scale=right[1][:],
+                start=True,
+                stop=True,
+            )
+
+        k1_t = load_list(k1, "k1_t")
+        offs_t = load_list(offs, "offs_t")
+        two_t = load_list(two, "two_t")
+
+        d_scale_table = held.tile([P, TABLE], U8, name="d_scale_table", align_bytes=64)
+        nc.vector.memset(d_scale_table[:].bitcast(I32), 0)
+        nc.sync.dma_start(d_scale_table[0:P:8, :].bitcast(I32), d_scales[0].bitcast(I32))
+        x_scale_table = held.tile([P, TABLE], U8, name="x_scale_table", align_bytes=64)
+        nc.vector.memset(x_scale_table[:].bitcast(I32), 0)
+        for q in range(4):
+            nc.sync.dma_start(
+                x_scale_table[32 * q : 32 * q + 4, :].bitcast(I32),
+                x_scales[0, 4 * q : 4 * q + 4, :].bitcast(I32),
+            )
+        d_scale_plane = held.tile([P, WIDTH], U8, name="d_scale_plane", align_bytes=64)
+        nc.gpsimd.memset(d_scale_plane[:].bitcast(I32), 0)
+
+        w1_raw = [load_weight_half(w1, half) for half in range(2)]
+        x_word_table = load_words(x_words, "x_word_table")
+        d_word_table = load_words(d_words, "d_word_table")
+        gn_t = held.tile([P, PACK], F32, name="gn_t")
+        nc.gpsimd.dma_start(gn_t[:], gn.rearrange("(p t) o -> p (t o)", t=PACK))
+        tau_t = held.tile([P, PACK], F32, name="tau_t")
+        nc.gpsimd.dma_start(tau_t[:], tau.rearrange("(p t) o -> p (t o)", t=PACK))
+
+        d_scale_picked = gather(d_scale_table, k1_t, U8, "d_scale_picked")
+        d_scale_dealt = deal(d_scale_picked, U8, "d_scale_dealt")
+        for q in range(4):
+            nc.sync.dma_start(
+                d_scale_plane[32 * q : 32 * q + 4, :].bitcast(I32),
+                d_scale_dealt[32 * q : 32 * q + 32 : 8, :].bitcast(I32),
+            )
+        n1_t = load_list(n1, "n1_t")
+        n2_t = load_list(n2, "n2_t")
+        n3_t = load_list(n3, "n3_t")
+        n4_t = load_list(n4, "n4_t")
+
+        x_offs_scales = gather(x_scale_table, offs_t, U8, "x_offs_scales")
+        x_two_scales = gather(x_scale_table, two_t, U8, "x_two_scales")
+
+        w1_grouped = held.tile([P, PACK * WIDTH], BF16, name="w1_grouped", align_bytes=64)
+        for half in range(2):
+            round_weight_half(w1_raw[half], w1_grouped, half)
+        w1_q = quantize(w1_grouped, WIDTH, "w1")
+        w2_raw = [load_weight_half(w2, half) for half in range(2)]
+
+        x_offs_words = gather(x_word_table, offs_t, U32, "x_offs_words")
+        y = []
+        for t in range(PACK):
+            acc = psum.tile([P, WIDTH], F32, name="acc")
+            product(acc[:], w1_q, t, (x_offs_words, x_offs_scales))
+            y_t = held.tile([P, WIDTH], F32, name=f"y{t}")
+            nc.scalar.copy(y_t[:], acc[:])
+            y.append(y_t)
+
+        x_two_words = gather(x_word_table, two_t, U32, "x_two_words")
+        gain = held.tile([P, PACK], F32, name="gain")
+        nc.vector.tensor_scalar(gain[:], gn_t[:], 0.75 * 0.0625, None, ALU.mult)
+        d_word_picked = gather(d_word_table, k1_t, U32, "d_word_picked")
+        d_word_dealt = deal(d_word_picked, U32, "d_word_dealt")
+
+        d_acc = []
+        for t in range(PACK):
+            acc = psum.tile([P, WIDTH], F32, name="acc")
+            product(acc[:], (d_word_dealt, d_scale_plane), t, (x_two_words, x_two_scales))
+            d_acc.append(acc)
+        d = [held.tile([P, WIDTH], F32, name=f"d{t}") for t in range(PACK)]
+
+        def empty_d(t):
+            if t == 0:
+                nc.vector.tensor_scalar(d[t][:], d_acc[t][:], gain[:, t : t + 1], None, ALU.mult)
+            else:
+                nc.scalar.activation(d[t][:], d_acc[t][:], ACT.Copy, scale=gain[:, t : t + 1])
+
+        def fetch(window, offsets, half, name):
+            tile = ring.tile([P, HALF], F32, name=name)
+            nc.scalar.activation(tile[:], window[:].indirect(half_list(offsets, half)), ACT.Copy)
+            return tile
+
+        def terms(t, half, first, second):
+            cols = half_cols(half)
+            if half == 1 and t >= FUSED_TILES:
+                d_n2 = fetch(d[t], n2_t, half, "d_n2")
+                nc.vector.tensor_tensor(first[:, t, :], d_n2[:], y[t][:, cols], ALU.mult)
+            else:
+                nc.vector.tensor_tensor(first[:, t, :], d[t][:].indirect(half_list(n2_t, half)), y[t][:, cols], ALU.mult)
+            y_n1 = fetch(y[t], n1_t, half, "y_n1")
+            nc.vector.tensor_tensor(second[:, t, :], y_n1[:], d[t][:, cols], ALU.mult)
+
+        z_q = []
+        w2_grouped = held.tile([P, PACK * WIDTH], BF16, name="w2_grouped", align_bytes=64)
+        w2_q = None
+        for half in range(2):
+            first = held.tile([P, PACK, HALF], F32, name=f"first{half}")
+            second = held.tile([P, PACK, HALF], F32, name=f"second{half}")
+            if half == 1:
+                for w_half in range(2):
+                    round_weight_half(w2_raw[w_half], w2_grouped, w_half)
+            for t in range(PACK):
+                if half == 0:
+                    empty_d(t)
+                terms(t, half, first, second)
+                if half == 1 and t == 1:
+                    w2_q = quantize(w2_grouped, WIDTH, "w2")
+            z = held.tile([P, PACK * HALF], BF16, name=f"z{half}", align_bytes=64)
+            nc.vector.tensor_tensor(
+                z[:].rearrange("p (c i t) -> p c t i", i=4, t=PACK),
+                first[:].rearrange("p t (c i) -> p c t i", i=4),
+                second[:].rearrange("p t (c i) -> p c t i", i=4),
+                ALU.subtract,
+            )
+            z_q.append(quantize(z, HALF, f"z{half}"))
+
+        h_acc = [psum.tile([P, WIDTH], F32, name="acc") for m in range(PACK)]
+        for half in range(2):
+            for m in range(PACK):
+                product(h_acc[m][:, half_cols(half)], w2_q, m, z_q[half])
+
+        out_rows = out.rearrange("(p t) c -> p t c", t=PACK)
+        h, bias, h_neg = [], [], []
+        for m in range(PACK):
+            h_m = held.tile([P, WIDTH], F32, name=f"h{m}")
+            top = held.tile([P, 1], F32, name=f"top{m}")
+            nc.vector.tensor_scalar(h_m[:], h_acc[m][:], 1.0, None, ALU.mult, ALU.max, accum_out=top[:])
+            bias_m = held.tile([P, 1], F32, name=f"bias{m}")
+            nc.vector.tensor_scalar(bias_m[:], top[:], tau_t[:, m : m + 1], -1.0, ALU.mult, ALU.mult)
+            h.append(h_m)
+            bias.append(bias_m)
+            if m < ADDING_TILES:
+                h_neg_m = held.tile([P, WIDTH], F32, name=f"h_neg{m}")
+                nc.gpsimd.tensor_scalar(h_neg_m[:], h_m[:], -0.5, 0.0, ALU.mult, ALU.add)
+                h_neg.append(h_neg_m)
+        for m in range(PACK):
+            ea = held.tile([P, WIDTH], F32, name=f"ea{m}")
+            larger = held.tile([P, WIDTH], F32, name=f"larger{m}")
+            result = held.tile([P, WIDTH], F32, name=f"result{m}")
+            h_n4 = [fetch(h[m], n4_t, half, "h_n4") for half in range(2)] if m >= ADDING_TILES else None
+            for half in range(2):
+                nc.scalar.activation(
+                    ea[:, half_cols(half)], h[m][:].indirect(half_list(n3_t, half)), ACT.Exp,
+                    bias=bias[m][:], scale=tau_t[:, m : m + 1],
+                )
+            for half in range(2):
+                cols = half_cols(half)
+                nc.vector.scalar_tensor_tensor(larger[:, cols], ea[:, cols], 2.0, h[m][:, cols], ALU.mult, ALU.max)
+            for half in range(2):
+                cols = half_cols(half)
+                if m < ADDING_TILES:
+                    nc.vector.tensor_tensor(
+                        result[:, cols], h_neg[m][:].indirect(half_list(n4_t, half)), larger[:, cols], ALU.add
+                    )
+                else:
+                    nc.vector.scalar_tensor_tensor(
+                        result[:, cols], h_n4[half][:], -0.5, larger[:, cols], ALU.mult, ALU.add
+                    )
+                if m == PACK - 1:
+                    nc.sync.dma_start(out_rows[:, m, cols], result[:, cols])
+            if m < PACK - 1:
+                nc.sync.dma_start(out_rows[:, m, :], result[:])

@@ -18,8 +18,10 @@ WIDTH = 512
 TABLE = 2048
 HALF = WIDTH // 2
 LIST_COLS = WIDTH // 16
-FUSED_TILES = 2
-ADDING_TILES = 2
+PARTS = (slice(0, 384), slice(384, 512))
+FUSED_TILES = (3, 1)
+ADDED = (1, 2, 0, 0)
+LAST_PIECES = (slice(0, 256), slice(256, 384), slice(384, 512))
 FLOPS = 3 * 2 * 512 * 512 * 512
 
 
@@ -38,16 +40,16 @@ def tile_picked_twkeycrossbecl_none_p_kernel(tc, x_words, x_scales, w1, d_words,
         def half_cols(half):
             return slice(half * HALF, (half + 1) * HALF)
 
-        def half_list(tile, half):
-            return tile[:, half * LIST_COLS // 2 : (half + 1) * LIST_COLS // 2]
+        def entries(tile, cols):
+            return tile[:, cols.start // 16 : cols.stop // 16]
 
         def load_words(src, name):
             tile = held.tile([P, TABLE], U32, name=name, align_bytes=64)
             nc.sync.dma_start(tile[:].bitcast(I32), src[0].rearrange("p n t -> p (n t)").bitcast(I32))
             return tile
 
-        def gather(window, offsets, dtype, name):
-            tile = held.tile([P, WIDTH], dtype, name=name, align_bytes=64)
+        def gather(window, offsets, dtype, name, tag=None):
+            tile = held.tile([P, WIDTH], dtype, name=name, tag=tag or name, align_bytes=64)
             nc.vector.tensor_copy(tile[:], window[:].indirect(offsets[:]))
             return tile
 
@@ -77,25 +79,22 @@ def tile_picked_twkeycrossbecl_none_p_kernel(tc, x_words, x_scales, w1, d_words,
             nc.vector.quantize_mx(out=codes[:].bitcast(FP8X4), scales=scales[:], in_=src[:])
             return codes, scales
 
-        def product(acc, left, t, right):
+        def product(acc, left, t, right, span=slice(0, WIDTH)):
             cols = slice(t * P, (t + 1) * P)
             nc.tensor.matmul_mx(
                 out=acc,
                 lhsT=left[0][:, cols].bitcast(FP8X4),
                 lhsT_scale=left[1][:, cols],
-                rhs=right[0][:].bitcast(FP8X4),
-                rhs_scale=right[1][:],
+                rhs=right[0][:, span].bitcast(FP8X4),
+                rhs_scale=right[1][:, span],
                 start=True,
                 stop=True,
             )
 
-        k1_t = load_list(k1, "k1_t")
         offs_t = load_list(offs, "offs_t")
         two_t = load_list(two, "two_t")
+        k1_t = load_list(k1, "k1_t")
 
-        d_scale_table = held.tile([P, TABLE], U8, name="d_scale_table", align_bytes=64)
-        nc.vector.memset(d_scale_table[:].bitcast(I32), 0)
-        nc.sync.dma_start(d_scale_table[0:P:8, :].bitcast(I32), d_scales[0].bitcast(I32))
         x_scale_table = held.tile([P, TABLE], U8, name="x_scale_table", align_bytes=64)
         nc.vector.memset(x_scale_table[:].bitcast(I32), 0)
         for q in range(4):
@@ -103,17 +102,23 @@ def tile_picked_twkeycrossbecl_none_p_kernel(tc, x_words, x_scales, w1, d_words,
                 x_scale_table[32 * q : 32 * q + 4, :].bitcast(I32),
                 x_scales[0, 4 * q : 4 * q + 4, :].bitcast(I32),
             )
+        d_scale_table = held.tile([P, TABLE], U8, name="d_scale_table", align_bytes=64)
+        nc.vector.memset(d_scale_table[:].bitcast(I32), 0)
+        nc.sync.dma_start(d_scale_table[0:P:8, :].bitcast(I32), d_scales[0].bitcast(I32))
         d_scale_plane = held.tile([P, WIDTH], U8, name="d_scale_plane", align_bytes=64)
-        nc.gpsimd.memset(d_scale_plane[:].bitcast(I32), 0)
+        nc.vector.memset(d_scale_plane[:].bitcast(I32), 0)
 
-        w1_raw = [load_weight_half(w1, half) for half in range(2)]
+        n1_t = load_list(n1, "n1_t")
         x_word_table = load_words(x_words, "x_word_table")
+        w1_raw = [load_weight_half(w1, half) for half in range(2)]
         d_word_table = load_words(d_words, "d_word_table")
         gn_t = held.tile([P, PACK], F32, name="gn_t")
         nc.gpsimd.dma_start(gn_t[:], gn.rearrange("(p t) o -> p (t o)", t=PACK))
         tau_t = held.tile([P, PACK], F32, name="tau_t")
         nc.gpsimd.dma_start(tau_t[:], tau.rearrange("(p t) o -> p (t o)", t=PACK))
 
+        x_offs_scales = gather(x_scale_table, offs_t, U8, "x_offs_scales")
+        x_two_scales = gather(x_scale_table, two_t, U8, "x_two_scales")
         d_scale_picked = gather(d_scale_table, k1_t, U8, "d_scale_picked")
         d_scale_dealt = deal(d_scale_picked, U8, "d_scale_dealt")
         for q in range(4):
@@ -121,130 +126,155 @@ def tile_picked_twkeycrossbecl_none_p_kernel(tc, x_words, x_scales, w1, d_words,
                 d_scale_plane[32 * q : 32 * q + 4, :].bitcast(I32),
                 d_scale_dealt[32 * q : 32 * q + 32 : 8, :].bitcast(I32),
             )
-        n1_t = load_list(n1, "n1_t")
         n2_t = load_list(n2, "n2_t")
         n3_t = load_list(n3, "n3_t")
         n4_t = load_list(n4, "n4_t")
 
-        x_offs_scales = gather(x_scale_table, offs_t, U8, "x_offs_scales")
-        x_two_scales = gather(x_scale_table, two_t, U8, "x_two_scales")
 
-        w1_grouped = held.tile([P, PACK * WIDTH], BF16, name="w1_grouped", align_bytes=64)
+        x_offs_words = gather(x_word_table, offs_t, U32, "x_offs_words")
+        x_two_words = gather(x_word_table, two_t, U32, "x_two_words")
+        gain = held.tile([P, PACK], F32, name="gain")
+        nc.scalar.mul(gain[:], gn_t[:], 0.75 * 0.0625)
+        w1_grouped = held.tile([P, PACK * WIDTH], BF16, name="w1_grouped", tag="picked", align_bytes=64)
         for half in range(2):
             round_weight_half(w1_raw[half], w1_grouped, half)
         w1_q = quantize(w1_grouped, WIDTH, "w1")
         w2_raw = [load_weight_half(w2, half) for half in range(2)]
 
-        x_offs_words = gather(x_word_table, offs_t, U32, "x_offs_words")
-        y = []
-        for t in range(PACK):
-            acc = psum.tile([P, WIDTH], F32, name="acc")
-            product(acc[:], w1_q, t, (x_offs_words, x_offs_scales))
-            y_t = held.tile([P, WIDTH], F32, name=f"y{t}")
-            nc.scalar.copy(y_t[:], acc[:])
-            y.append(y_t)
-
-        x_two_words = gather(x_word_table, two_t, U32, "x_two_words")
-        gain = held.tile([P, PACK], F32, name="gain")
-        nc.vector.tensor_scalar(gain[:], gn_t[:], 0.75 * 0.0625, None, ALU.mult)
-        d_word_picked = gather(d_word_table, k1_t, U32, "d_word_picked")
-        d_word_dealt = deal(d_word_picked, U32, "d_word_dealt")
-
-        d_acc = []
-        for t in range(PACK):
-            acc = psum.tile([P, WIDTH], F32, name="acc")
-            product(acc[:], (d_word_dealt, d_scale_plane), t, (x_two_words, x_two_scales))
-            d_acc.append(acc)
+        y = [held.tile([P, WIDTH], F32, name=f"y{t}") for t in range(PACK)]
         d = [held.tile([P, WIDTH], F32, name=f"d{t}") for t in range(PACK)]
 
-        def empty_d(t):
-            if t == 0:
-                nc.vector.tensor_scalar(d[t][:], d_acc[t][:], gain[:, t : t + 1], None, ALU.mult)
-            else:
-                nc.scalar.activation(d[t][:], d_acc[t][:], ACT.Copy, scale=gain[:, t : t + 1])
+        def make_y(t):
+            acc = psum.tile([P, WIDTH], F32, name="acc")
+            product(acc[:], w1_q, t, (x_offs_words, x_offs_scales))
+            nc.scalar.copy(y[t][:], acc[:])
 
-        def fetch(window, offsets, half, name):
-            tile = ring.tile([P, HALF], F32, name=name)
-            nc.scalar.activation(tile[:], window[:].indirect(half_list(offsets, half)), ACT.Copy)
+        def make_d(t):
+            acc = psum.tile([P, WIDTH], F32, name="acc")
+            product(acc[:], (d_word_dealt, d_scale_plane), t, (x_two_words, x_two_scales))
+            nc.scalar.activation(d[t][:], acc[:], ACT.Copy, scale=gain[:, t : t + 1])
+
+        d_word_picked = gather(d_word_table, k1_t, U32, "d_word_picked", "picked")
+        d_word_dealt = deal(d_word_picked, U32, "d_word_dealt")
+        y0_n1 = held.tile([P, WIDTH], F32, name="y0_n1", tag="picked", align_bytes=64)
+        make_y(0)
+        for cols in PARTS:
+            nc.vector.tensor_copy(y0_n1[:, cols], y[0][:].indirect(entries(n1_t, cols)))
+        make_y(1)
+
+        def fetch(window, offsets, cols, name):
+            tile = ring.tile([P, cols.stop - cols.start], F32, name=name)
+            nc.scalar.activation(tile[:], window[:].indirect(entries(offsets, cols)), ACT.Copy)
             return tile
 
-        def terms(t, half, first, second):
-            cols = half_cols(half)
-            if half == 1 and t >= FUSED_TILES:
-                d_n2 = fetch(d[t], n2_t, half, "d_n2")
+        def terms(t, part, first, second):
+            cols = PARTS[part]
+            if part == 0:
+                make_d(t)
+                if t + 2 < PACK:
+                    make_y(t + 2)
+            y_n1 = y0_n1[:, cols] if t == 0 else fetch(y[t], n1_t, cols, "y_n1")[:]
+            if t >= FUSED_TILES[part]:
+                d_n2 = fetch(d[t], n2_t, cols, "d_n2")
                 nc.vector.tensor_tensor(first[:, t, :], d_n2[:], y[t][:, cols], ALU.mult)
             else:
-                nc.vector.tensor_tensor(first[:, t, :], d[t][:].indirect(half_list(n2_t, half)), y[t][:, cols], ALU.mult)
-            y_n1 = fetch(y[t], n1_t, half, "y_n1")
-            nc.vector.tensor_tensor(second[:, t, :], y_n1[:], d[t][:, cols], ALU.mult)
+                nc.vector.tensor_tensor(first[:, t, :], d[t][:].indirect(entries(n2_t, cols)), y[t][:, cols], ALU.mult)
+            nc.vector.tensor_tensor(second[:, t, :], y_n1, d[t][:, cols], ALU.mult)
 
         z_q = []
         w2_grouped = held.tile([P, PACK * WIDTH], BF16, name="w2_grouped", align_bytes=64)
         w2_q = None
-        for half in range(2):
-            first = held.tile([P, PACK, HALF], F32, name=f"first{half}")
-            second = held.tile([P, PACK, HALF], F32, name=f"second{half}")
-            if half == 1:
+        for part, cols in enumerate(PARTS):
+            width = cols.stop - cols.start
+            first = held.tile([P, PACK, width], F32, name=f"first{part}")
+            second = held.tile([P, PACK, width], F32, name=f"second{part}")
+            for t in range(PACK):
+                terms(t, part, first, second)
+            if part == 0:
                 for w_half in range(2):
                     round_weight_half(w2_raw[w_half], w2_grouped, w_half)
-            for t in range(PACK):
-                if half == 0:
-                    empty_d(t)
-                terms(t, half, first, second)
-                if half == 1 and t == 1:
-                    w2_q = quantize(w2_grouped, WIDTH, "w2")
-            z = held.tile([P, PACK * HALF], BF16, name=f"z{half}", align_bytes=64)
+            z = held.tile([P, PACK * width], BF16, name=f"z{part}", align_bytes=64)
             nc.vector.tensor_tensor(
                 z[:].rearrange("p (c i t) -> p c t i", i=4, t=PACK),
                 first[:].rearrange("p t (c i) -> p c t i", i=4),
                 second[:].rearrange("p t (c i) -> p c t i", i=4),
                 ALU.subtract,
             )
-            z_q.append(quantize(z, HALF, f"z{half}"))
+            z_q.append(quantize(z, width, f"z{part}"))
+            if part == 0:
+                w2_q = quantize(w2_grouped, WIDTH, "w2")
 
         h_acc = [psum.tile([P, WIDTH], F32, name="acc") for m in range(PACK)]
-        for half in range(2):
-            for m in range(PACK):
-                product(h_acc[m][:, half_cols(half)], w2_q, m, z_q[half])
+        for m in range(PACK):
+            product(h_acc[m][:, 0:256], w2_q, m, z_q[0], slice(0, 256))
+            product(h_acc[m][:, 256:384], w2_q, m, z_q[0], slice(256, 384))
+        for m in range(PACK):
+            product(h_acc[m][:, 384:512], w2_q, m, z_q[1], slice(0, 128))
 
         out_rows = out.rearrange("(p t) c -> p t c", t=PACK)
-        h, bias, h_neg = [], [], []
+        halves = [half_cols(half) for half in range(2)]
+        h, bias, h_neg, h_n4 = [], [], {}, {}
         for m in range(PACK):
             h_m = held.tile([P, WIDTH], F32, name=f"h{m}")
             top = held.tile([P, 1], F32, name=f"top{m}")
             nc.vector.tensor_scalar(h_m[:], h_acc[m][:], 1.0, None, ALU.mult, ALU.max, accum_out=top[:])
             bias_m = held.tile([P, 1], F32, name=f"bias{m}")
-            nc.vector.tensor_scalar(bias_m[:], top[:], tau_t[:, m : m + 1], -1.0, ALU.mult, ALU.mult)
+            nc.gpsimd.tensor_scalar(bias_m[:], top[:], tau_t[:, m : m + 1], -1.0, ALU.mult, ALU.mult)
             h.append(h_m)
             bias.append(bias_m)
-            if m < ADDING_TILES:
-                h_neg_m = held.tile([P, WIDTH], F32, name=f"h_neg{m}")
-                nc.gpsimd.tensor_scalar(h_neg_m[:], h_m[:], -0.5, 0.0, ALU.mult, ALU.add)
-                h_neg.append(h_neg_m)
+            if ADDED[m]:
+                h_neg[m] = held.tile([P, WIDTH], F32, name=f"h_neg{m}")
+                nc.gpsimd.tensor_scalar(h_neg[m][:], h_m[:], -0.5, 0.0, ALU.mult, ALU.add)
+        def fetch_h(m, cols):
+            nc.scalar.activation(h_n4[m][:, cols], h[m][:].indirect(entries(n4_t, cols)), ACT.Copy)
+
+        def exponential(m, cols):
+            nc.scalar.activation(
+                ea[m][:, cols], h[m][:].indirect(entries(n3_t, cols)), ACT.Exp,
+                bias=bias[m][:], scale=tau_t[:, m : m + 1],
+            )
+
+        def take_larger(m, cols):
+            nc.vector.scalar_tensor_tensor(larger[m][:, cols], ea[m][:, cols], 2.0, h[m][:, cols], ALU.mult, ALU.max)
+
+        def add_fetched(m, cols):
+            nc.vector.tensor_tensor(
+                result[m][:, cols], h_neg[m][:].indirect(entries(n4_t, cols)), larger[m][:, cols], ALU.add
+            )
+
+        def add_plain(m, cols):
+            nc.vector.scalar_tensor_tensor(
+                result[m][:, cols], h_n4[m][:, cols], -0.5, larger[m][:, cols], ALU.mult, ALU.add
+            )
+
+        ea = [held.tile([P, WIDTH], F32, name=f"ea{m}") for m in range(PACK)]
+        larger = [held.tile([P, WIDTH], F32, name=f"larger{m}") for m in range(PACK)]
+        result = [held.tile([P, WIDTH], F32, name=f"result{m}") for m in range(PACK)]
         for m in range(PACK):
-            ea = held.tile([P, WIDTH], F32, name=f"ea{m}")
-            larger = held.tile([P, WIDTH], F32, name=f"larger{m}")
-            result = held.tile([P, WIDTH], F32, name=f"result{m}")
-            h_n4 = [fetch(h[m], n4_t, half, "h_n4") for half in range(2)] if m >= ADDING_TILES else None
-            for half in range(2):
-                nc.scalar.activation(
-                    ea[:, half_cols(half)], h[m][:].indirect(half_list(n3_t, half)), ACT.Exp,
-                    bias=bias[m][:], scale=tau_t[:, m : m + 1],
-                )
-            for half in range(2):
-                cols = half_cols(half)
-                nc.vector.scalar_tensor_tensor(larger[:, cols], ea[:, cols], 2.0, h[m][:, cols], ALU.mult, ALU.max)
-            for half in range(2):
-                cols = half_cols(half)
-                if m < ADDING_TILES:
-                    nc.vector.tensor_tensor(
-                        result[:, cols], h_neg[m][:].indirect(half_list(n4_t, half)), larger[:, cols], ALU.add
-                    )
-                else:
-                    nc.vector.scalar_tensor_tensor(
-                        result[:, cols], h_n4[half][:], -0.5, larger[:, cols], ALU.mult, ALU.add
-                    )
-                if m == PACK - 1:
-                    nc.sync.dma_start(out_rows[:, m, cols], result[:, cols])
-            if m < PACK - 1:
-                nc.sync.dma_start(out_rows[:, m, :], result[:])
+            if ADDED[m] < 2:
+                h_n4[m] = held.tile([P, WIDTH], F32, name=f"h_n4_{m}")
+        for m in range(PACK - 1):
+            if m == 0:
+                for cols in halves[ADDED[m] :]:
+                    fetch_h(m, cols)
+            for cols in halves:
+                exponential(m, cols)
+            if m > 0:
+                for cols in halves[ADDED[m] :]:
+                    fetch_h(m, cols)
+            take_larger(m, slice(0, WIDTH))
+            for cols in halves[: ADDED[m]]:
+                add_fetched(m, cols)
+            if ADDED[m] < 2:
+                add_plain(m, slice(ADDED[m] * HALF, WIDTH))
+            nc.sync.dma_start(out_rows[:, m, :], result[m][:])
+        last = PACK - 1
+        for cols in halves:
+            exponential(last, cols)
+            take_larger(last, cols)
+        for cols in LAST_PIECES:
+            fetch_h(last, cols)
+            add_plain(last, cols)
+            if cols.stop % HALF == 0:
+                done = slice(cols.stop - HALF, cols.stop)
+                nc.sync.dma_start(out_rows[:, last, done], result[last][:, done])

@@ -19,7 +19,8 @@ TABLE = 2048
 HALF = WIDTH // 2
 LIST_COLS = WIDTH // 16
 PARTS = (slice(0, 384), slice(384, 512))
-FUSED_TILES = (3, 1)
+FUSED_TILES = (3, 2)
+EARLY = 1
 ADDED = (1, 2, 0, 0)
 LAST_PIECES = (slice(0, 256), slice(256, 384), slice(384, 512))
 FLOPS = 3 * 2 * 512 * 512 * 512
@@ -29,6 +30,7 @@ def tile_picked_twkeycrossbecl_none_p_kernel(tc, x_words, x_scales, w1, d_words,
     nc = tc.nc
     with ExitStack() as ctx:
         held = ctx.enter_context(tc.tile_pool(name="held", bufs=1))
+        reused = ctx.enter_context(tc.tile_pool(name="reused", bufs=1))
         ring = ctx.enter_context(tc.tile_pool(name="ring", bufs=PACK))
         psum = ctx.enter_context(tc.psum_pool(name="psum", bufs=8))
 
@@ -53,8 +55,13 @@ def tile_picked_twkeycrossbecl_none_p_kernel(tc, x_words, x_scales, w1, d_words,
             nc.vector.tensor_copy(tile[:], window[:].indirect(offsets[:]))
             return tile
 
+        def gather_at(place, window, offsets, dtype, name):
+            tile = reused.tile([P, WIDTH], dtype, name=name, align_bytes=64, offset=place)
+            nc.vector.tensor_copy(tile[:], window[:].indirect(offsets[:]))
+            return tile
+
         def deal(src, dtype, name):
-            tile = held.tile([P, WIDTH], dtype, name=name, align_bytes=64)
+            tile = held.tile([P, WIDTH], dtype, name=name, tag=name, align_bytes=64)
             nc.vector.tensor_copy(
                 tile[:].rearrange("p (t m) -> p m t", t=PACK),
                 src[:].rearrange("p (m t) -> p m t", t=PACK),
@@ -92,8 +99,8 @@ def tile_picked_twkeycrossbecl_none_p_kernel(tc, x_words, x_scales, w1, d_words,
             )
 
         offs_t = load_list(offs, "offs_t")
-        two_t = load_list(two, "two_t")
         k1_t = load_list(k1, "k1_t")
+        two_t = load_list(two, "two_t")
 
         x_scale_table = held.tile([P, TABLE], U8, name="x_scale_table", align_bytes=64)
         nc.vector.memset(x_scale_table[:].bitcast(I32), 0)
@@ -102,15 +109,19 @@ def tile_picked_twkeycrossbecl_none_p_kernel(tc, x_words, x_scales, w1, d_words,
                 x_scale_table[32 * q : 32 * q + 4, :].bitcast(I32),
                 x_scales[0, 4 * q : 4 * q + 4, :].bitcast(I32),
             )
+        w1_raw = held.tile([P, PACK, WIDTH], F32, name="w1_raw")
+        nc.sync.dma_start(w1_raw[:], w1.rearrange("(p j) c -> p j c", j=PACK))
         d_scale_table = held.tile([P, TABLE], U8, name="d_scale_table", align_bytes=64)
         nc.vector.memset(d_scale_table[:].bitcast(I32), 0)
         nc.sync.dma_start(d_scale_table[0:P:8, :].bitcast(I32), d_scales[0].bitcast(I32))
         d_scale_plane = held.tile([P, WIDTH], U8, name="d_scale_plane", align_bytes=64)
         nc.vector.memset(d_scale_plane[:].bitcast(I32), 0)
 
-        n1_t = load_list(n1, "n1_t")
         x_word_table = load_words(x_words, "x_word_table")
-        w1_raw = [load_weight_half(w1, half) for half in range(2)]
+        n1_t = load_list(n1, "n1_t")
+        n2_t = load_list(n2, "n2_t")
+        n3_t = load_list(n3, "n3_t")
+        n4_t = load_list(n4, "n4_t")
         d_word_table = load_words(d_words, "d_word_table")
         gn_t = held.tile([P, PACK], F32, name="gn_t")
         nc.gpsimd.dma_start(gn_t[:], gn.rearrange("(p t) o -> p (t o)", t=PACK))
@@ -119,32 +130,37 @@ def tile_picked_twkeycrossbecl_none_p_kernel(tc, x_words, x_scales, w1, d_words,
 
         x_offs_scales = gather(x_scale_table, offs_t, U8, "x_offs_scales")
         x_two_scales = gather(x_scale_table, two_t, U8, "x_two_scales")
-        d_scale_picked = gather(d_scale_table, k1_t, U8, "d_scale_picked")
+        d_scale_picked = gather(d_scale_table, k1_t, U8, "d_scale_picked", "w2_slot")
         d_scale_dealt = deal(d_scale_picked, U8, "d_scale_dealt")
         for q in range(4):
             nc.sync.dma_start(
                 d_scale_plane[32 * q : 32 * q + 4, :].bitcast(I32),
                 d_scale_dealt[32 * q : 32 * q + 32 : 8, :].bitcast(I32),
             )
-        n2_t = load_list(n2, "n2_t")
-        n3_t = load_list(n3, "n3_t")
-        n4_t = load_list(n4, "n4_t")
+        w2_raw = held.tile([P, PACK, WIDTH], F32, name="w2_raw", tag="w2_slot", align_bytes=64)
+        nc.sync.dma_start(w2_raw[:], w2.rearrange("(p j) c -> p j c", j=PACK))
 
-
-        x_offs_words = gather(x_word_table, offs_t, U32, "x_offs_words")
-        x_two_words = gather(x_word_table, two_t, U32, "x_two_words")
         gain = held.tile([P, PACK], F32, name="gain")
-        nc.scalar.mul(gain[:], gn_t[:], 0.75 * 0.0625)
-        w1_grouped = held.tile([P, PACK * WIDTH], BF16, name="w1_grouped", tag="picked", align_bytes=64)
-        for half in range(2):
-            round_weight_half(w1_raw[half], w1_grouped, half)
+        nc.gpsimd.tensor_scalar(gain[:], gn_t[:], 0.75 * 0.0625, 0.0, ALU.mult, ALU.add)
+        w1_grouped = reused.tile([P, PACK * WIDTH], BF16, name="w1_grouped", align_bytes=64, offset=0)
+        nc.scalar.copy(
+            w1_grouped[:].rearrange("p (t m j) -> p m j t", t=PACK, j=PACK),
+            w1_raw[:].rearrange("p j (m t) -> p m j t", t=PACK),
+        )
+        x_offs_words = gather(x_word_table, offs_t, U32, "x_offs_words")
         w1_q = quantize(w1_grouped, WIDTH, "w1")
-        w2_raw = [load_weight_half(w2, half) for half in range(2)]
+        x_two_words = gather_at(0, x_word_table, two_t, U32, "x_two_words")
+        d_word_picked = gather_at(4096, d_word_table, k1_t, U32, "d_word_picked")
+        d_word_dealt = deal(d_word_picked, U32, "d_word_dealt")
+        w2_grouped = reused.tile([P, PACK * WIDTH], BF16, name="w2_grouped", align_bytes=64, offset=4096)
+        nc.vector.tensor_copy(
+            w2_grouped[:].rearrange("p (t m j) -> p m j t", t=PACK, j=PACK),
+            w2_raw[:].rearrange("p j (m t) -> p m j t", t=PACK),
+        )
 
         y = [held.tile([P, WIDTH], F32, name=f"y{t}") for t in range(PACK)]
         d = [held.tile([P, WIDTH], F32, name=f"d{t}") for t in range(PACK)]
-
-        def make_y(t):
+        for t in range(PACK):
             acc = psum.tile([P, WIDTH], F32, name="acc")
             product(acc[:], w1_q, t, (x_offs_words, x_offs_scales))
             nc.scalar.copy(y[t][:], acc[:])
@@ -154,62 +170,59 @@ def tile_picked_twkeycrossbecl_none_p_kernel(tc, x_words, x_scales, w1, d_words,
             product(acc[:], (d_word_dealt, d_scale_plane), t, (x_two_words, x_two_scales))
             nc.scalar.activation(d[t][:], acc[:], ACT.Copy, scale=gain[:, t : t + 1])
 
-        d_word_picked = gather(d_word_table, k1_t, U32, "d_word_picked", "picked")
-        d_word_dealt = deal(d_word_picked, U32, "d_word_dealt")
-        y0_n1 = held.tile([P, WIDTH], F32, name="y0_n1", tag="picked", align_bytes=64)
-        make_y(0)
-        for cols in PARTS:
-            nc.vector.tensor_copy(y0_n1[:, cols], y[0][:].indirect(entries(n1_t, cols)))
-        make_y(1)
+        def fetch(target, window, offsets, cols):
+            nc.scalar.activation(target, window[:].indirect(entries(offsets, cols)), ACT.Copy)
 
-        def fetch(window, offsets, cols, name):
-            tile = ring.tile([P, cols.stop - cols.start], F32, name=name)
-            nc.scalar.activation(tile[:], window[:].indirect(entries(offsets, cols)), ACT.Copy)
-            return tile
+        early = held.tile([P, EARLY, HALF], F32, name="y_n1_early")
+        for t in range(EARLY):
+            fetch(early[:, t, :], y[t], n1_t, half_cols(0))
+        for t in range(2):
+            make_d(t)
 
-        def terms(t, part, first, second):
-            cols = PARTS[part]
-            if part == 0:
+        def terms(t, part, first, second, late):
+            cols = half_cols(part)
+            if part == 0 and t >= 2:
                 make_d(t)
-                if t + 2 < PACK:
-                    make_y(t + 2)
-            y_n1 = y0_n1[:, cols] if t == 0 else fetch(y[t], n1_t, cols, "y_n1")[:]
             if t >= FUSED_TILES[part]:
-                d_n2 = fetch(d[t], n2_t, cols, "d_n2")
+                d_n2 = ring.tile([P, HALF], F32, name="d_n2")
+                fetch(d_n2[:], d[t], n2_t, cols)
+            if part == 0 and t < EARLY:
+                y_n1 = early[:, t, :]
+            else:
+                y_n1 = late(t)
+                fetch(y_n1, y[t], n1_t, cols)
+            if t >= FUSED_TILES[part]:
+                nc.vector.tensor_tensor(second[:, t, :], y_n1, d[t][:, cols], ALU.mult)
                 nc.vector.tensor_tensor(first[:, t, :], d_n2[:], y[t][:, cols], ALU.mult)
             else:
                 nc.vector.tensor_tensor(first[:, t, :], d[t][:].indirect(entries(n2_t, cols)), y[t][:, cols], ALU.mult)
-            nc.vector.tensor_tensor(second[:, t, :], y_n1, d[t][:, cols], ALU.mult)
+                nc.vector.tensor_tensor(second[:, t, :], y_n1, d[t][:, cols], ALU.mult)
 
         z_q = []
-        w2_grouped = held.tile([P, PACK * WIDTH], BF16, name="w2_grouped", align_bytes=64)
         w2_q = None
-        for part, cols in enumerate(PARTS):
-            width = cols.stop - cols.start
-            first = held.tile([P, PACK, width], F32, name=f"first{part}")
-            second = held.tile([P, PACK, width], F32, name=f"second{part}")
+        late_a = held.tile([P, PACK, HALF], F32, name="y_n1_late_a", tag="d_word_dealt", align_bytes=64)
+        late_b = held.tile([P, PACK, HALF], F32, name="y_n1_late_b", tag="x_two_scales", align_bytes=64)
+        lates = (lambda t: late_a[:, t, :], lambda t: late_b[:, t, :])
+        for part in range(2):
+            first = held.tile([P, PACK, HALF], F32, name=f"first{part}")
+            second = held.tile([P, PACK, HALF], F32, name=f"second{part}")
             for t in range(PACK):
-                terms(t, part, first, second)
-            if part == 0:
-                for w_half in range(2):
-                    round_weight_half(w2_raw[w_half], w2_grouped, w_half)
-            z = held.tile([P, PACK * width], BF16, name=f"z{part}", align_bytes=64)
+                terms(t, part, first, second, lates[part])
+                if (part, t) == (0, 1):
+                    w2_q = quantize(w2_grouped, WIDTH, "w2")
+            z = held.tile([P, PACK * HALF], BF16, name=f"z{part}", align_bytes=64)
             nc.vector.tensor_tensor(
                 z[:].rearrange("p (c i t) -> p c t i", i=4, t=PACK),
                 first[:].rearrange("p t (c i) -> p c t i", i=4),
                 second[:].rearrange("p t (c i) -> p c t i", i=4),
                 ALU.subtract,
             )
-            z_q.append(quantize(z, width, f"z{part}"))
-            if part == 0:
-                w2_q = quantize(w2_grouped, WIDTH, "w2")
+            z_q.append(quantize(z, HALF, f"z{part}"))
 
         h_acc = [psum.tile([P, WIDTH], F32, name="acc") for m in range(PACK)]
-        for m in range(PACK):
-            product(h_acc[m][:, 0:256], w2_q, m, z_q[0], slice(0, 256))
-            product(h_acc[m][:, 256:384], w2_q, m, z_q[0], slice(256, 384))
-        for m in range(PACK):
-            product(h_acc[m][:, 384:512], w2_q, m, z_q[1], slice(0, 128))
+        for part in range(2):
+            for m in range(PACK):
+                product(h_acc[m][:, half_cols(part)], w2_q, m, z_q[part], slice(0, HALF))
 
         out_rows = out.rearrange("(p t) c -> p t c", t=PACK)
         halves = [half_cols(half) for half in range(2)]
@@ -275,6 +288,4 @@ def tile_picked_twkeycrossbecl_none_p_kernel(tc, x_words, x_scales, w1, d_words,
         for cols in LAST_PIECES:
             fetch_h(last, cols)
             add_plain(last, cols)
-            if cols.stop % HALF == 0:
-                done = slice(cols.stop - HALF, cols.stop)
-                nc.sync.dma_start(out_rows[:, last, done], result[last][:, done])
+            nc.sync.dma_start(out_rows[:, last, cols], result[last][:, cols])

@@ -16,48 +16,62 @@ P = 128
 PACK = 4
 WIDTH = 512
 TABLE = 2048
+GROUP = 16
+QUADRANTS = 4
+BANKS = 8
+
 HALF = WIDTH // 2
-LIST_COLS = WIDTH // 16
-PARTS = (slice(0, 384), slice(384, 512))
-FUSED_TILES = (3, 2)
-EARLY = 1
-ADDED = (1, 2, 0, 0)
-LAST_PIECES = (slice(0, 256), slice(256, 384), slice(384, 512))
+HALVES = (slice(0, HALF), slice(HALF, WIDTH))
+PARTS = (slice(0, 384), slice(384, WIDTH))
+SPANS = ((0, slice(0, 256)), (0, slice(256, 384)), (1, slice(0, 128)))
+FUSED_TILES = (3, 0)
+EARLY_TILES = (1, 2)
+FUSED_HALVES = (1, 2, 0)
+LAST_PIECES = (slice(0, 256), slice(256, 384), slice(384, WIDTH))
+
 FLOPS = 3 * 2 * 512 * 512 * 512
 
 
-def tile_picked_twkeycrossbecl_none_p_kernel(tc, x_words, x_scales, w1, d_words, d_scales, gn, w2, tau, offs, k1, two, n1, n2, n3, n4, out):
+def tile_picked_twkeycrossbecl_none_p_kernel(
+    tc, x_words, x_scales, w1, d_words, d_scales, gn, w2, tau, offs, k1, two, n1, n2, n3, n4, out
+):
     nc = tc.nc
     with ExitStack() as ctx:
         held = ctx.enter_context(tc.tile_pool(name="held", bufs=1))
-        reused = ctx.enter_context(tc.tile_pool(name="reused", bufs=1))
         ring = ctx.enter_context(tc.tile_pool(name="ring", bufs=PACK))
-        psum = ctx.enter_context(tc.psum_pool(name="psum", bufs=8))
+        psum = ctx.enter_context(tc.psum_pool(name="psum", bufs=BANKS))
 
         def load_list(src, name):
-            tile = held.tile([P, LIST_COLS], U16, name=name)
+            tile = held.tile([P, WIDTH // GROUP], U16, name=name)
             nc.sync.dma_start(tile[:], src)
             return tile
 
-        def half_cols(half):
-            return slice(half * HALF, (half + 1) * HALF)
-
-        def entries(tile, cols):
-            return tile[:, cols.start // 16 : cols.stop // 16]
+        def entries(offsets, cols):
+            return offsets[:, cols.start // GROUP : cols.stop // GROUP]
 
         def load_words(src, name):
             tile = held.tile([P, TABLE], U32, name=name, align_bytes=64)
             nc.sync.dma_start(tile[:].bitcast(I32), src[0].rearrange("p n t -> p (n t)").bitcast(I32))
             return tile
 
-        def gather(window, offsets, dtype, name, tag=None):
-            tile = held.tile([P, WIDTH], dtype, name=name, tag=tag or name, align_bytes=64)
-            nc.vector.tensor_copy(tile[:], window[:].indirect(offsets[:]))
+        def zeroed_bytes(width, name):
+            tile = held.tile([P, width], U8, name=name, align_bytes=64)
+            nc.vector.memset(tile[:].bitcast(I32), 0)
             return tile
 
-        def gather_at(place, window, offsets, dtype, name):
-            tile = reused.tile([P, WIDTH], dtype, name=name, align_bytes=64, offset=place)
-            nc.vector.tensor_copy(tile[:], window[:].indirect(offsets[:]))
+        def load_weight(w, name, tag):
+            raw = held.tile([P, PACK, WIDTH], F32, name=name, tag=tag, align_bytes=64)
+            nc.sync.dma_start(raw[:], w.rearrange("(p j) c -> p j c", j=PACK))
+            return raw
+
+        def load_row_values(src, name):
+            tile = held.tile([P, PACK], F32, name=name)
+            nc.gpsimd.dma_start(tile[:], src.rearrange("(p t) o -> p (t o)", t=PACK))
+            return tile
+
+        def gather_packed(table, offsets, dtype, name, tag):
+            tile = held.tile([P, WIDTH], dtype, name=name, tag=tag, align_bytes=64)
+            nc.vector.tensor_copy(tile[:], table[:].indirect(offsets[:]))
             return tile
 
         def deal(src, dtype, name):
@@ -68,15 +82,9 @@ def tile_picked_twkeycrossbecl_none_p_kernel(tc, x_words, x_scales, w1, d_words,
             )
             return tile
 
-        def load_weight_half(w, half):
-            raw = held.tile([P, PACK, HALF], F32, name=f"w_raw{half}")
-            nc.sync.dma_start(raw[:], w[:, half_cols(half)].rearrange("(p j) c -> p j c", j=PACK))
-            return raw
-
-        def round_weight_half(raw, grouped, half):
-            span = P // 2
+        def round_weight(raw, rounded):
             nc.scalar.copy(
-                grouped[:].rearrange("p (t m j) -> p m j t", t=PACK, j=PACK)[:, half * span : (half + 1) * span],
+                rounded[:].rearrange("p (t m j) -> p m j t", t=PACK, j=PACK),
                 raw[:].rearrange("p j (m t) -> p m j t", t=PACK),
             )
 
@@ -86,36 +94,37 @@ def tile_picked_twkeycrossbecl_none_p_kernel(tc, x_words, x_scales, w1, d_words,
             nc.vector.quantize_mx(out=codes[:].bitcast(FP8X4), scales=scales[:], in_=src[:])
             return codes, scales
 
-        def product(acc, left, t, right, span=slice(0, WIDTH)):
-            cols = slice(t * P, (t + 1) * P)
+        def product(acc, left, t, right, span):
+            places = slice(t * P, (t + 1) * P)
             nc.tensor.matmul_mx(
                 out=acc,
-                lhsT=left[0][:, cols].bitcast(FP8X4),
-                lhsT_scale=left[1][:, cols],
+                lhsT=left[0][:, places].bitcast(FP8X4),
+                lhsT_scale=left[1][:, places],
                 rhs=right[0][:, span].bitcast(FP8X4),
                 rhs_scale=right[1][:, span],
                 start=True,
                 stop=True,
             )
 
+        def fetch(target, window, offsets, cols):
+            nc.scalar.activation(target, window[:].indirect(entries(offsets, cols)), ACT.Copy)
+
+        whole = slice(0, WIDTH)
+
         offs_t = load_list(offs, "offs_t")
         k1_t = load_list(k1, "k1_t")
         two_t = load_list(two, "two_t")
 
-        x_scale_table = held.tile([P, TABLE], U8, name="x_scale_table", align_bytes=64)
-        nc.vector.memset(x_scale_table[:].bitcast(I32), 0)
-        for q in range(4):
+        x_scale_table = zeroed_bytes(TABLE, "x_scale_table")
+        for q in range(QUADRANTS):
             nc.sync.dma_start(
                 x_scale_table[32 * q : 32 * q + 4, :].bitcast(I32),
                 x_scales[0, 4 * q : 4 * q + 4, :].bitcast(I32),
             )
-        w1_raw = held.tile([P, PACK, WIDTH], F32, name="w1_raw")
-        nc.sync.dma_start(w1_raw[:], w1.rearrange("(p j) c -> p j c", j=PACK))
-        d_scale_table = held.tile([P, TABLE], U8, name="d_scale_table", align_bytes=64)
-        nc.vector.memset(d_scale_table[:].bitcast(I32), 0)
+        w1_raw = load_weight(w1, "w1_raw", "w1_raw")
+        d_scale_table = zeroed_bytes(TABLE, "d_scale_table")
         nc.sync.dma_start(d_scale_table[0:P:8, :].bitcast(I32), d_scales[0].bitcast(I32))
-        d_scale_plane = held.tile([P, WIDTH], U8, name="d_scale_plane", align_bytes=64)
-        nc.vector.memset(d_scale_plane[:].bitcast(I32), 0)
+        d_scale_placed = zeroed_bytes(WIDTH, "d_scale_placed")
 
         x_word_table = load_words(x_words, "x_word_table")
         n1_t = load_list(n1, "n1_t")
@@ -123,110 +132,106 @@ def tile_picked_twkeycrossbecl_none_p_kernel(tc, x_words, x_scales, w1, d_words,
         n3_t = load_list(n3, "n3_t")
         n4_t = load_list(n4, "n4_t")
         d_word_table = load_words(d_words, "d_word_table")
-        gn_t = held.tile([P, PACK], F32, name="gn_t")
-        nc.gpsimd.dma_start(gn_t[:], gn.rearrange("(p t) o -> p (t o)", t=PACK))
-        tau_t = held.tile([P, PACK], F32, name="tau_t")
-        nc.gpsimd.dma_start(tau_t[:], tau.rearrange("(p t) o -> p (t o)", t=PACK))
+        gn_t = load_row_values(gn, "gn_t")
+        tau_t = load_row_values(tau, "tau_t")
 
-        x_offs_scales = gather(x_scale_table, offs_t, U8, "x_offs_scales")
-        x_two_scales = gather(x_scale_table, two_t, U8, "x_two_scales")
-        d_scale_picked = gather(d_scale_table, k1_t, U8, "d_scale_picked", "w2_slot")
+        x_offs_scales = gather_packed(x_scale_table, offs_t, U8, "x_offs_scales", "x_offs_scales")
+        x_two_scales = gather_packed(x_scale_table, two_t, U8, "x_two_scales", "x_two_scales")
+        d_scale_picked = gather_packed(d_scale_table, k1_t, U8, "d_scale_picked", "w2_raw")
         d_scale_dealt = deal(d_scale_picked, U8, "d_scale_dealt")
-        for q in range(4):
+        for q in range(QUADRANTS):
             nc.sync.dma_start(
-                d_scale_plane[32 * q : 32 * q + 4, :].bitcast(I32),
+                d_scale_placed[32 * q : 32 * q + 4, :].bitcast(I32),
                 d_scale_dealt[32 * q : 32 * q + 32 : 8, :].bitcast(I32),
             )
-        w2_raw = held.tile([P, PACK, WIDTH], F32, name="w2_raw", tag="w2_slot", align_bytes=64)
-        nc.sync.dma_start(w2_raw[:], w2.rearrange("(p j) c -> p j c", j=PACK))
+        w2_raw = load_weight(w2, "w2_raw", "w2_raw")
 
         gain = held.tile([P, PACK], F32, name="gain")
         nc.gpsimd.tensor_scalar(gain[:], gn_t[:], 0.75 * 0.0625, 0.0, ALU.mult, ALU.add)
-        w1_grouped = reused.tile([P, PACK * WIDTH], BF16, name="w1_grouped", align_bytes=64, offset=0)
-        nc.scalar.copy(
-            w1_grouped[:].rearrange("p (t m j) -> p m j t", t=PACK, j=PACK),
-            w1_raw[:].rearrange("p j (m t) -> p m j t", t=PACK),
-        )
-        x_offs_words = gather(x_word_table, offs_t, U32, "x_offs_words")
-        w1_q = quantize(w1_grouped, WIDTH, "w1")
-        x_two_words = gather_at(0, x_word_table, two_t, U32, "x_two_words")
-        d_word_picked = gather_at(4096, d_word_table, k1_t, U32, "d_word_picked")
+        w1_rounded = held.tile([P, PACK * WIDTH], BF16, name="w1_rounded", tag="rounded", align_bytes=64)
+        round_weight(w1_raw, w1_rounded)
+        x_offs_words = gather_packed(x_word_table, offs_t, U32, "x_offs_words", "x_offs_words")
+        w1_q = quantize(w1_rounded, WIDTH, "w1")
+        x_two_words = gather_packed(x_word_table, two_t, U32, "x_two_words", "rounded")
+        d_word_picked = gather_packed(d_word_table, k1_t, U32, "d_word_picked", "d_word_picked")
         d_word_dealt = deal(d_word_picked, U32, "d_word_dealt")
-        w2_grouped = reused.tile([P, PACK * WIDTH], BF16, name="w2_grouped", align_bytes=64, offset=4096)
-        nc.vector.tensor_copy(
-            w2_grouped[:].rearrange("p (t m j) -> p m j t", t=PACK, j=PACK),
-            w2_raw[:].rearrange("p j (m t) -> p m j t", t=PACK),
-        )
 
         y = [held.tile([P, WIDTH], F32, name=f"y{t}") for t in range(PACK)]
         d = [held.tile([P, WIDTH], F32, name=f"d{t}") for t in range(PACK)]
         for t in range(PACK):
             acc = psum.tile([P, WIDTH], F32, name="acc")
-            product(acc[:], w1_q, t, (x_offs_words, x_offs_scales))
+            product(acc[:], w1_q, t, (x_offs_words, x_offs_scales), whole)
             nc.scalar.copy(y[t][:], acc[:])
 
         def make_d(t):
             acc = psum.tile([P, WIDTH], F32, name="acc")
-            product(acc[:], (d_word_dealt, d_scale_plane), t, (x_two_words, x_two_scales))
+            product(acc[:], (d_word_dealt, d_scale_placed), t, (x_two_words, x_two_scales), whole)
             nc.scalar.activation(d[t][:], acc[:], ACT.Copy, scale=gain[:, t : t + 1])
 
-        def fetch(target, window, offsets, cols):
-            nc.scalar.activation(target, window[:].indirect(entries(offsets, cols)), ACT.Copy)
-
-        early = held.tile([P, EARLY, HALF], F32, name="y_n1_early")
-        for t in range(EARLY):
-            fetch(early[:, t, :], y[t], n1_t, half_cols(0))
-        for t in range(2):
+        y_n1 = {}
+        y0_n1 = held.tile([P, WIDTH], F32, name="y0_n1", tag="d_word_picked", align_bytes=64)
+        for part, cols in enumerate(PARTS):
+            nc.vector.tensor_copy(y0_n1[:, cols], y[0][:].indirect(entries(n1_t, cols)))
+            y_n1[0, part] = y0_n1[:, cols]
+        short = len(PARTS) - 1
+        for t in EARLY_TILES:
+            early = held.tile([P, PARTS[short].stop - PARTS[short].start], F32, name=f"y_n1_early{t}")
+            fetch(early[:], y[t], n1_t, PARTS[short])
+            y_n1[t, short] = early[:]
+        late = held.tile([P, PACK - 1, WIDTH], F32, name="y_n1_late", tag="d_word_dealt", align_bytes=64)
+        ahead = 2
+        for t in range(ahead):
             make_d(t)
 
-        def terms(t, part, first, second, late):
-            cols = half_cols(part)
-            if part == 0 and t >= 2:
+        def terms(t, part, first, second):
+            cols = PARTS[part]
+            fused = t < FUSED_TILES[part]
+            if part == 0 and t >= ahead:
                 make_d(t)
-            if t >= FUSED_TILES[part]:
-                d_n2 = ring.tile([P, HALF], F32, name="d_n2")
+            if not fused:
+                d_n2 = ring.tile([P, cols.stop - cols.start], F32, name="d_n2")
                 fetch(d_n2[:], d[t], n2_t, cols)
-            if part == 0 and t < EARLY:
-                y_n1 = early[:, t, :]
-            else:
-                y_n1 = late(t)
-                fetch(y_n1, y[t], n1_t, cols)
-            if t >= FUSED_TILES[part]:
-                nc.vector.tensor_tensor(second[:, t, :], y_n1, d[t][:, cols], ALU.mult)
-                nc.vector.tensor_tensor(first[:, t, :], d_n2[:], y[t][:, cols], ALU.mult)
-            else:
-                nc.vector.tensor_tensor(first[:, t, :], d[t][:].indirect(entries(n2_t, cols)), y[t][:, cols], ALU.mult)
-                nc.vector.tensor_tensor(second[:, t, :], y_n1, d[t][:, cols], ALU.mult)
+            if (t, part) not in y_n1:
+                y_n1[t, part] = late[:, t - 1, cols]
+                fetch(y_n1[t, part], y[t], n1_t, cols)
+            looked_up = d[t][:].indirect(entries(n2_t, cols)) if fused else d_n2[:]
+            nc.vector.tensor_tensor(first[:, t, :], looked_up, y[t][:, cols], ALU.mult)
+            nc.vector.tensor_tensor(second[:, t, :], y_n1[t, part], d[t][:, cols], ALU.mult)
 
-        z_q = []
-        w2_q = None
-        late_a = held.tile([P, PACK, HALF], F32, name="y_n1_late_a", tag="d_word_dealt", align_bytes=64)
-        late_b = held.tile([P, PACK, HALF], F32, name="y_n1_late_b", tag="x_two_scales", align_bytes=64)
-        lates = (lambda t: late_a[:, t, :], lambda t: late_b[:, t, :])
-        for part in range(2):
-            first = held.tile([P, PACK, HALF], F32, name=f"first{part}")
-            second = held.tile([P, PACK, HALF], F32, name=f"second{part}")
+        def make_terms(part):
+            width = PARTS[part].stop - PARTS[part].start
+            first = held.tile([P, PACK, width], F32, name=f"first{part}")
+            second = held.tile([P, PACK, width], F32, name=f"second{part}")
             for t in range(PACK):
-                terms(t, part, first, second, lates[part])
-                if (part, t) == (0, 1):
-                    w2_q = quantize(w2_grouped, WIDTH, "w2")
-            z = held.tile([P, PACK * HALF], BF16, name=f"z{part}", align_bytes=64)
+                terms(t, part, first, second)
+            return first, second
+
+        def make_z(part, first, second):
+            width = PARTS[part].stop - PARTS[part].start
+            z = held.tile([P, PACK * width], BF16, name=f"z{part}", align_bytes=64)
             nc.vector.tensor_tensor(
                 z[:].rearrange("p (c i t) -> p c t i", i=4, t=PACK),
                 first[:].rearrange("p t (c i) -> p c t i", i=4),
                 second[:].rearrange("p t (c i) -> p c t i", i=4),
                 ALU.subtract,
             )
-            z_q.append(quantize(z, HALF, f"z{part}"))
+            return quantize(z, width, f"z{part}")
+
+        w2_rounded = held.tile([P, PACK * WIDTH], BF16, name="w2_rounded", tag="rounded", align_bytes=64)
+        long_terms = make_terms(0)
+        round_weight(w2_raw, w2_rounded)
+        z_q = [make_z(0, *long_terms)]
+        w2_q = quantize(w2_rounded, WIDTH, "w2")
+        z_q.append(make_z(short, *make_terms(short)))
 
         h_acc = [psum.tile([P, WIDTH], F32, name="acc") for m in range(PACK)]
-        for part in range(2):
-            for m in range(PACK):
-                product(h_acc[m][:, half_cols(part)], w2_q, m, z_q[part], slice(0, HALF))
+        for m in range(PACK):
+            for part, span in SPANS:
+                start = PARTS[part].start
+                product(h_acc[m][:, start + span.start : start + span.stop], w2_q, m, z_q[part], span)
 
-        out_rows = out.rearrange("(p t) c -> p t c", t=PACK)
-        halves = [half_cols(half) for half in range(2)]
-        h, bias, h_neg, h_n4 = [], [], {}, {}
+        last = PACK - 1
+        h, bias, h_neg = [], [], {}
         for m in range(PACK):
             h_m = held.tile([P, WIDTH], F32, name=f"h{m}")
             top = held.tile([P, 1], F32, name=f"top{m}")
@@ -235,57 +240,65 @@ def tile_picked_twkeycrossbecl_none_p_kernel(tc, x_words, x_scales, w1, d_words,
             nc.gpsimd.tensor_scalar(bias_m[:], top[:], tau_t[:, m : m + 1], -1.0, ALU.mult, ALU.mult)
             h.append(h_m)
             bias.append(bias_m)
-            if ADDED[m]:
+            if m < last and FUSED_HALVES[m]:
                 h_neg[m] = held.tile([P, WIDTH], F32, name=f"h_neg{m}")
                 nc.gpsimd.tensor_scalar(h_neg[m][:], h_m[:], -0.5, 0.0, ALU.mult, ALU.add)
+
+        ea = [held.tile([P, WIDTH], F32, name=f"ea{m}") for m in range(PACK)]
+        larger = [held.tile([P, WIDTH], F32, name=f"larger{m}") for m in range(PACK)]
+        result = [held.tile([P, WIDTH], F32, name=f"result{m}") for m in range(PACK)]
+        h_n4 = {
+            m: held.tile([P, WIDTH], F32, name=f"h_n4_{m}")
+            for m in range(PACK)
+            if m == last or FUSED_HALVES[m] < len(HALVES)
+        }
+        out_rows = out.rearrange("(p t) c -> p t c", t=PACK)
+
         def fetch_h(m, cols):
-            nc.scalar.activation(h_n4[m][:, cols], h[m][:].indirect(entries(n4_t, cols)), ACT.Copy)
+            fetch(h_n4[m][:, cols], h[m], n4_t, cols)
 
         def exponential(m, cols):
             nc.scalar.activation(
-                ea[m][:, cols], h[m][:].indirect(entries(n3_t, cols)), ACT.Exp,
-                bias=bias[m][:], scale=tau_t[:, m : m + 1],
+                ea[m][:, cols],
+                h[m][:].indirect(entries(n3_t, cols)),
+                ACT.Exp,
+                bias=bias[m][:],
+                scale=tau_t[:, m : m + 1],
             )
 
         def take_larger(m, cols):
             nc.vector.scalar_tensor_tensor(larger[m][:, cols], ea[m][:, cols], 2.0, h[m][:, cols], ALU.mult, ALU.max)
 
-        def add_fetched(m, cols):
+        def add_fused(m, cols):
             nc.vector.tensor_tensor(
                 result[m][:, cols], h_neg[m][:].indirect(entries(n4_t, cols)), larger[m][:, cols], ALU.add
             )
 
-        def add_plain(m, cols):
+        def add_fetched(m, cols):
             nc.vector.scalar_tensor_tensor(
                 result[m][:, cols], h_n4[m][:, cols], -0.5, larger[m][:, cols], ALU.mult, ALU.add
             )
 
-        ea = [held.tile([P, WIDTH], F32, name=f"ea{m}") for m in range(PACK)]
-        larger = [held.tile([P, WIDTH], F32, name=f"larger{m}") for m in range(PACK)]
-        result = [held.tile([P, WIDTH], F32, name=f"result{m}") for m in range(PACK)]
-        for m in range(PACK):
-            if ADDED[m] < 2:
-                h_n4[m] = held.tile([P, WIDTH], F32, name=f"h_n4_{m}")
-        for m in range(PACK - 1):
+        for m in range(last):
+            fused_halves, fetched_halves = HALVES[: FUSED_HALVES[m]], HALVES[FUSED_HALVES[m] :]
+            steps = [(exponential, cols) for cols in HALVES] + [(fetch_h, cols) for cols in fetched_halves]
             if m == 0:
-                for cols in halves[ADDED[m] :]:
-                    fetch_h(m, cols)
-            for cols in halves:
-                exponential(m, cols)
-            if m > 0:
-                for cols in halves[ADDED[m] :]:
-                    fetch_h(m, cols)
-            take_larger(m, slice(0, WIDTH))
-            for cols in halves[: ADDED[m]]:
-                add_fetched(m, cols)
-            if ADDED[m] < 2:
-                add_plain(m, slice(ADDED[m] * HALF, WIDTH))
+                steps = steps[len(HALVES) :] + steps[: len(HALVES)]
+            for step, cols in steps:
+                step(m, cols)
+            take_larger(m, whole)
+            for cols in fused_halves:
+                add_fused(m, cols)
+            if fetched_halves:
+                add_fetched(m, slice(fetched_halves[0].start, WIDTH))
             nc.sync.dma_start(out_rows[:, m, :], result[m][:])
-        last = PACK - 1
-        for cols in halves:
+
+        for cols in HALVES:
             exponential(last, cols)
             take_larger(last, cols)
         for cols in LAST_PIECES:
             fetch_h(last, cols)
-            add_plain(last, cols)
-            nc.sync.dma_start(out_rows[:, last, cols], result[last][:, cols])
+            add_fetched(last, cols)
+            if cols.stop % HALF == 0:
+                done = slice(cols.stop - HALF, cols.stop)
+                nc.sync.dma_start(out_rows[:, last, done], result[last][:, done])

from contextlib import ExitStack

import concourse.mybir as mybir

F32 = mybir.dt.float32
BF16 = mybir.dt.bfloat16
I32 = mybir.dt.int32
U32 = mybir.dt.uint32
U16 = mybir.dt.uint16
U8 = mybir.dt.uint8
FP8X4 = mybir.dt.float8_e4m3fn_x4
ALU = mybir.AluOpType
ACT = mybir.ActivationFunctionType

P = 128
PACK = 4
WIDTH = 512
TABLE = 2048
GROUP = 16
QUADRANTS = 4
BANKS = 8

HALF = WIDTH // 2
HALVES = (slice(0, HALF), slice(HALF, WIDTH))
PARTS = (slice(0, 384), slice(384, WIDTH))
SPANS = ((0, slice(0, 256)), (0, slice(256, 384)), (1, slice(0, 128)))
FUSED_TILES = (3, 0)
EARLY_TILES = (1, 2)
FUSED_HALVES = (1, 2, 0)
LAST_PIECES = (slice(0, 256), slice(256, 384), slice(384, WIDTH))

FLOPS = 3 * 2 * 512 * 512 * 512


def tile_picked_twkeycrossbecl_none_p_kernel(
    tc, x_words, x_scales, w1, d_words, d_scales, gn, w2, tau, offs, k1, two, n1, n2, n3, n4, out
):
    nc = tc.nc
    with ExitStack() as ctx:
        held = ctx.enter_context(tc.tile_pool(name="held", bufs=1))
        ring = ctx.enter_context(tc.tile_pool(name="ring", bufs=PACK))
        psum = ctx.enter_context(tc.psum_pool(name="psum", bufs=BANKS))

        def load_list(src, name):
            tile = held.tile([P, WIDTH // GROUP], U16, name=name)
            nc.sync.dma_start(tile[:], src)
            return tile

        def entries(offsets, cols):
            return offsets[:, cols.start // GROUP : cols.stop // GROUP]

        def load_words(src, name):
            tile = held.tile([P, TABLE], U32, name=name, align_bytes=64)
            nc.sync.dma_start(tile[:].bitcast(I32), src[0].rearrange("p n t -> p (n t)").bitcast(I32))
            return tile

        def zeroed_bytes(width, name):
            tile = held.tile([P, width], U8, name=name, align_bytes=64)
            nc.vector.memset(tile[:].bitcast(I32), 0)
            return tile

        def load_weight(w, name, tag):
            raw = held.tile([P, PACK, WIDTH], F32, name=name, tag=tag, align_bytes=64)
            nc.sync.dma_start(raw[:], w.rearrange("(p j) c -> p j c", j=PACK))
            return raw

        def load_row_values(src, name):
            tile = held.tile([P, PACK], F32, name=name)
            nc.gpsimd.dma_start(tile[:], src.rearrange("(p t) o -> p (t o)", t=PACK))
            return tile

        def gather_packed(table, offsets, dtype, name, tag):
            tile = held.tile([P, WIDTH], dtype, name=name, tag=tag, align_bytes=64)
            nc.vector.tensor_copy(tile[:], table[:].indirect(offsets[:]))
            return tile

        def deal(src, dtype, name):
            tile = held.tile([P, WIDTH], dtype, name=name, tag=name, align_bytes=64)
            nc.vector.tensor_copy(
                tile[:].rearrange("p (t m) -> p m t", t=PACK),
                src[:].rearrange("p (m t) -> p m t", t=PACK),
            )
            return tile

        def round_weight(raw, rounded):
            nc.scalar.copy(
                rounded[:].rearrange("p (t m j) -> p m j t", t=PACK, j=PACK),
                raw[:].rearrange("p j (m t) -> p m j t", t=PACK),
            )

        def quantize(src, width, name):
            codes = held.tile([P, width], U32, name=name + "_codes", align_bytes=64)
            scales = held.tile([P, width], U8, name=name + "_scales", align_bytes=64)
            nc.vector.quantize_mx(out=codes[:].bitcast(FP8X4), scales=scales[:], in_=src[:])
            return codes, scales

        def product(acc, left, t, right, span):
            places = slice(t * P, (t + 1) * P)
            nc.tensor.matmul_mx(
                out=acc,
                lhsT=left[0][:, places].bitcast(FP8X4),
                lhsT_scale=left[1][:, places],
                rhs=right[0][:, span].bitcast(FP8X4),
                rhs_scale=right[1][:, span],
                start=True,
                stop=True,
            )

        def fetch(target, window, offsets, cols):
            nc.scalar.activation(target, window[:].indirect(entries(offsets, cols)), ACT.Copy)

        whole = slice(0, WIDTH)

        offs_t = load_list(offs, "offs_t")
        k1_t = load_list(k1, "k1_t")
        two_t = load_list(two, "two_t")

        x_scale_table = zeroed_bytes(TABLE, "x_scale_table")
        for q in range(QUADRANTS):
            nc.sync.dma_start(
                x_scale_table[32 * q : 32 * q + 4, :].bitcast(I32),
                x_scales[0, 4 * q : 4 * q + 4, :].bitcast(I32),
            )
        w1_raw = load_weight(w1, "w1_raw", "w1_raw")
        d_scale_table = zeroed_bytes(TABLE, "d_scale_table")
        nc.sync.dma_start(d_scale_table[0:P:8, :].bitcast(I32), d_scales[0].bitcast(I32))
        d_scale_placed = zeroed_bytes(WIDTH, "d_scale_placed")

        x_word_table = load_words(x_words, "x_word_table")
        n1_t = load_list(n1, "n1_t")
        n2_t = load_list(n2, "n2_t")
        n3_t = load_list(n3, "n3_t")
        n4_t = load_list(n4, "n4_t")
        d_word_table = load_words(d_words, "d_word_table")
        gn_t = load_row_values(gn, "gn_t")
        tau_t = load_row_values(tau, "tau_t")

        x_offs_scales = gather_packed(x_scale_table, offs_t, U8, "x_offs_scales", "x_offs_scales")
        x_two_scales = gather_packed(x_scale_table, two_t, U8, "x_two_scales", "x_two_scales")
        d_scale_picked = gather_packed(d_scale_table, k1_t, U8, "d_scale_picked", "w2_raw")
        d_scale_dealt = deal(d_scale_picked, U8, "d_scale_dealt")
        for q in range(QUADRANTS):
            nc.sync.dma_start(
                d_scale_placed[32 * q : 32 * q + 4, :].bitcast(I32),
                d_scale_dealt[32 * q : 32 * q + 32 : 8, :].bitcast(I32),
            )
        w2_raw = load_weight(w2, "w2_raw", "w2_raw")

        gain = held.tile([P, PACK], F32, name="gain")
        nc.gpsimd.tensor_scalar(gain[:], gn_t[:], 0.75 * 0.0625, 0.0, ALU.mult, ALU.add)
        w1_rounded = held.tile([P, PACK * WIDTH], BF16, name="w1_rounded", tag="rounded", align_bytes=64)
        round_weight(w1_raw, w1_rounded)
        x_offs_words = gather_packed(x_word_table, offs_t, U32, "x_offs_words", "x_offs_words")
        w1_q = quantize(w1_rounded, WIDTH, "w1")
        x_two_words = gather_packed(x_word_table, two_t, U32, "x_two_words", "rounded")
        d_word_picked = gather_packed(d_word_table, k1_t, U32, "d_word_picked", "d_word_picked")
        d_word_dealt = deal(d_word_picked, U32, "d_word_dealt")

        y = [held.tile([P, WIDTH], F32, name=f"y{t}") for t in range(PACK)]
        d = [held.tile([P, WIDTH], F32, name=f"d{t}") for t in range(PACK)]
        for t in range(PACK):
            acc = psum.tile([P, WIDTH], F32, name="acc")
            product(acc[:], w1_q, t, (x_offs_words, x_offs_scales), whole)
            nc.scalar.copy(y[t][:], acc[:])

        def make_d(t):
            acc = psum.tile([P, WIDTH], F32, name="acc")
            product(acc[:], (d_word_dealt, d_scale_placed), t, (x_two_words, x_two_scales), whole)
            nc.scalar.activation(d[t][:], acc[:], ACT.Copy, scale=gain[:, t : t + 1])

        y_n1 = {}
        y0_n1 = held.tile([P, WIDTH], F32, name="y0_n1", tag="d_word_picked", align_bytes=64)
        for part, cols in enumerate(PARTS):
            nc.vector.tensor_copy(y0_n1[:, cols], y[0][:].indirect(entries(n1_t, cols)))
            y_n1[0, part] = y0_n1[:, cols]
        short = len(PARTS) - 1
        for t in EARLY_TILES:
            early = held.tile([P, PARTS[short].stop - PARTS[short].start], F32, name=f"y_n1_early{t}")
            fetch(early[:], y[t], n1_t, PARTS[short])
            y_n1[t, short] = early[:]
        late = held.tile([P, PACK - 1, WIDTH], F32, name="y_n1_late", tag="d_word_dealt", align_bytes=64)
        ahead = 2
        for t in range(ahead):
            make_d(t)

        def terms(t, part, first, second):
            cols = PARTS[part]
            fused = t < FUSED_TILES[part]
            if part == 0 and t >= ahead:
                make_d(t)
            if not fused:
                d_n2 = ring.tile([P, cols.stop - cols.start], F32, name="d_n2")
                fetch(d_n2[:], d[t], n2_t, cols)
            if (t, part) not in y_n1:
                y_n1[t, part] = late[:, t - 1, cols]
                fetch(y_n1[t, part], y[t], n1_t, cols)
            looked_up = d[t][:].indirect(entries(n2_t, cols)) if fused else d_n2[:]
            nc.vector.tensor_tensor(first[:, t, :], looked_up, y[t][:, cols], ALU.mult)
            nc.vector.tensor_tensor(second[:, t, :], y_n1[t, part], d[t][:, cols], ALU.mult)

        def make_terms(part):
            width = PARTS[part].stop - PARTS[part].start
            first = held.tile([P, PACK, width], F32, name=f"first{part}")
            second = held.tile([P, PACK, width], F32, name=f"second{part}")
            for t in range(PACK):
                terms(t, part, first, second)
            return first, second

        def make_z(part, first, second):
            width = PARTS[part].stop - PARTS[part].start
            z = held.tile([P, PACK * width], BF16, name=f"z{part}", align_bytes=64)
            nc.vector.tensor_tensor(
                z[:].rearrange("p (c i t) -> p c t i", i=4, t=PACK),
                first[:].rearrange("p t (c i) -> p c t i", i=4),
                second[:].rearrange("p t (c i) -> p c t i", i=4),
                ALU.subtract,
            )
            return quantize(z, width, f"z{part}")

        w2_rounded = held.tile([P, PACK * WIDTH], BF16, name="w2_rounded", tag="rounded", align_bytes=64)
        long_terms = make_terms(0)
        round_weight(w2_raw, w2_rounded)
        z_q = [make_z(0, *long_terms)]
        w2_q = quantize(w2_rounded, WIDTH, "w2")
        z_q.append(make_z(short, *make_terms(short)))

        h_acc = [psum.tile([P, WIDTH], F32, name="acc") for m in range(PACK)]
        for m in range(PACK):
            for part, span in SPANS:
                start = PARTS[part].start
                product(h_acc[m][:, start + span.start : start + span.stop], w2_q, m, z_q[part], span)

        last = PACK - 1
        h, bias, h_neg = [], [], {}
        for m in range(PACK):
            h_m = held.tile([P, WIDTH], F32, name=f"h{m}")
            top = held.tile([P, 1], F32, name=f"top{m}")
            nc.vector.tensor_scalar(h_m[:], h_acc[m][:], 1.0, None, ALU.mult, ALU.max, accum_out=top[:])
            bias_m = held.tile([P, 1], F32, name=f"bias{m}")
            nc.gpsimd.tensor_scalar(bias_m[:], top[:], tau_t[:, m : m + 1], -1.0, ALU.mult, ALU.mult)
            h.append(h_m)
            bias.append(bias_m)
            if m < last and FUSED_HALVES[m]:
                h_neg[m] = held.tile([P, WIDTH], F32, name=f"h_neg{m}")
                nc.gpsimd.tensor_scalar(h_neg[m][:], h_m[:], -0.5, 0.0, ALU.mult, ALU.add)

        ea = [held.tile([P, WIDTH], F32, name=f"ea{m}") for m in range(PACK)]
        larger = [held.tile([P, WIDTH], F32, name=f"larger{m}") for m in range(PACK)]
        result = [held.tile([P, WIDTH], F32, name=f"result{m}") for m in range(PACK)]
        h_n4 = {
            m: held.tile([P, WIDTH], F32, name=f"h_n4_{m}")
            for m in range(PACK)
            if m == last or FUSED_HALVES[m] < len(HALVES)
        }
        out_rows = out.rearrange("(p t) c -> p t c", t=PACK)

        def fetch_h(m, cols):
            fetch(h_n4[m][:, cols], h[m], n4_t, cols)

        def exponential(m, cols):
            nc.scalar.activation(
                ea[m][:, cols],
                h[m][:].indirect(entries(n3_t, cols)),
                ACT.Exp,
                bias=bias[m][:],
                scale=tau_t[:, m : m + 1],
            )

        def take_larger(m, cols):
            nc.vector.scalar_tensor_tensor(larger[m][:, cols], ea[m][:, cols], 2.0, h[m][:, cols], ALU.mult, ALU.max)

        def add_fused(m, cols):
            nc.vector.tensor_tensor(
                result[m][:, cols], h_neg[m][:].indirect(entries(n4_t, cols)), larger[m][:, cols], ALU.add
            )

        def add_fetched(m, cols):
            nc.vector.scalar_tensor_tensor(
                result[m][:, cols], h_n4[m][:, cols], -0.5, larger[m][:, cols], ALU.mult, ALU.add
            )

        for m in range(last):
            fused_halves, fetched_halves = HALVES[: FUSED_HALVES[m]], HALVES[FUSED_HALVES[m] :]
            steps = [(exponential, cols) for cols in HALVES] + [(fetch_h, cols) for cols in fetched_halves]
            if m == 0:
                steps = steps[len(HALVES) :] + steps[: len(HALVES)]
            for step, cols in steps:
                step(m, cols)
            take_larger(m, whole)
            for cols in fused_halves:
                add_fused(m, cols)
            if fetched_halves:
                add_fetched(m, slice(fetched_halves[0].start, WIDTH))
            nc.sync.dma_start(out_rows[:, m, :], result[m][:])

        for cols in HALVES:
            exponential(last, cols)
            take_larger(last, cols)
        for cols in LAST_PIECES:
            fetch_h(last, cols)
            add_fetched(last, cols)
            if cols.stop % HALF == 0:
                done = slice(cols.stop - HALF, cols.stop)
                nc.sync.dma_start(out_rows[:, last, done], result[last][:, done])
